import numpy as np
import ml_dtypes


def mxq(x, axis, fmt="e4m3"):
    dtype, down = {"e4m3": (ml_dtypes.float8_e4m3fn, 7), "e5m2": (ml_dtypes.float8_e5m2, 14)}[fmt]
    v = np.moveaxis(np.asarray(x, np.float32).astype(ml_dtypes.bfloat16).astype(np.float64), axis, -1)
    blocks = v.reshape(v.shape[:-1] + (-1, 32))
    amax = np.abs(blocks).max(-1, keepdims=True)
    byte = np.maximum(np.where(amax > 0, np.frexp(amax)[1] - 1 + 127, 0) - down, 1)
    scale = np.exp2(byte - 127.0)
    codes = (blocks / scale).astype(np.float32).astype(dtype).astype(np.float64)
    return np.moveaxis((codes * scale).reshape(v.shape), -1, axis)


WIDE = False


def mx_kscale(k):
    if not WIDE:
        return np.ones(k)
    levels = np.array([10, -10, 5, -5, 0])
    if k % 512:
        return np.exp2(np.random.permutation(np.resize(levels, k // 32))).repeat(32)
    a = np.empty((k // 512, 16))
    for p in range(k // 512):
        a[p, :8] = np.random.permutation(np.resize(levels, 8))
        for g in range(8):
            far = levels[np.abs(levels - a[p, g]) >= 10]
            a[p, g + 8] = far[np.random.randint(len(far))]
    return np.exp2(a.ravel()).repeat(32)


def f64(x):
    return np.asarray(x).astype(np.float64)


def striped(idx):
    return np.tile(idx.reshape(-1, 16).T, (8, 1)).astype(np.uint16)


def unstriped(offs):
    return offs[:16].T.reshape(-1).astype(np.int64)


E2M1 = np.array([0.0, 0.5, 1.0, 1.5, 2.0, 3.0, 4.0, 6.0, -0.0, -0.5, -1.0, -1.5, -2.0, -3.0, -4.0, -6.0])


def pack_weight(w, fmt):
    k, n = w.shape
    w = f64(np.asarray(w, np.float32).astype(ml_dtypes.bfloat16)).reshape(k // 32, 32, n)
    amax = np.abs(w).max(1)
    if fmt == "e4m3":
        byte = np.frexp(amax)[1] - 1 + 127 - 7
    else:
        mant, ex = np.frexp(amax / 6.0)
        byte = np.where(mant > 0.5, ex, ex - 1) + 127
    byte = np.clip(np.where(amax > 0, byte, 1), 1, 254)
    scaled = (w * np.exp2(127.0 - byte)[:, None, :]).reshape(k, n).astype(np.float32)
    by_word = np.ascontiguousarray(scaled.reshape(k // 512, 128, 4, n).transpose(0, 1, 3, 2))
    if fmt == "e4m3":
        words = by_word.astype(ml_dtypes.float8_e4m3fn).view(np.uint8)
    else:
        c = by_word.astype(ml_dtypes.float4_e2m1fn).view(np.uint8) & 0xF
        words = (c[..., 0::2] | (c[..., 1::2] << 4)).reshape(k // 512, 128, 2 * n)
    return np.ascontiguousarray(words), np.ascontiguousarray(byte.astype(np.uint8).reshape(k // 512, 16, n))


def unpack_weight(words, scales, fmt):
    g, _, n = scales.shape
    words = np.ascontiguousarray(words).reshape(g, 128, n, -1)
    if fmt == "e4m3":
        vals = words.view(ml_dtypes.float8_e4m3fn).astype(np.float64)
    else:
        nib = np.empty((g, 128, n, 4), np.uint8)
        nib[..., 0::2] = words & 0xF
        nib[..., 1::2] = words >> 4
        vals = E2M1[nib]
    vals = vals * np.repeat(np.exp2(scales.astype(np.float64) - 127.0), 8, axis=1)[..., None]
    return vals.transpose(0, 1, 3, 2).reshape(g * 512, n)


def pack_table(v):
    words, scales = pack_weight(v, "e4m3")
    return np.concatenate([words.reshape(words.shape[0], -1), scales.reshape(scales.shape[0], -1)], axis=1)


def unpack_table(tab):
    g, t = tab.shape[0], tab.shape[1] // 528
    return unpack_weight(tab[:, :512 * t].reshape(g, 128, t, 4), tab[:, 512 * t:].reshape(g, 16, t), "e4m3")


G, K, M, T, S = 2, 512, 512, 2048, 256


def setup_inputs():
    n = np.random.standard_normal
    s = mx_kscale(K)[:, None]
    return {
        "tab": pack_table(n((K, T)) * s),
        "w": (n((K, M)) / np.sqrt(K) / s).astype(np.float32),
        "r": (n((256, 512))).astype(np.float32),
        "offs": striped(np.concatenate([np.random.permutation(T)[:S] for _ in range(G)])),
    }


def reference(tab, w, r, offs):
    tab_ = unpack_table(tab)[:, unstriped(offs).reshape(G, S)].sum(1)
    w_ = mxq(f64(w), 0, "e4m3")
    y = tab_.T @ w_
    return f64(r) + y

@@ -1,0 +1,98 @@
+from contextlib import ExitStack
+
+import concourse.mybir as mybir
+
+G, K, M, T, S = 2, 512, 512, 2048, 256
+FLOPS = 2 * G * K * M * S
+
+F32 = mybir.dt.float32
+BF16 = mybir.dt.bfloat16
+I32 = mybir.dt.int32
+U32 = mybir.dt.uint32
+U16 = mybir.dt.uint16
+U8 = mybir.dt.uint8
+FP8X4 = mybir.dt.float8_e4m3fn_x4
+ADD = mybir.AluOpType.add
+
+P = 128
+PACK = 4
+J_TILES = S // P
+LOAD_COLS = 256
+CHUNK = 128
+
+
+def tile_list_tabbag_tm_res_kernel(tc, tab, w, r, offs, out):
+    nc = tc.nc
+    with ExitStack() as ctx:
+        keep = ctx.enter_context(tc.tile_pool(name="keep", bufs=1))
+        psum = ctx.enter_context(tc.psum_pool(name="psum", bufs=1))
+
+        offsets = keep.tile([P, G * S // 16], U16, name="offsets")
+        nc.sync.dma_start(offsets[:], offs)
+
+        table_words = keep.tile([P, T], I32, name="table_words")
+        nc.sync.dma_start(table_words[:], tab[0, 0 : K * T].rearrange("(p b) -> p b", p=P).bitcast(I32))
+
+        table_scales = keep.tile([P, T], U8, name="table_scales")
+        nc.vector.memset(table_scales[:].bitcast(I32), 0)
+        scale_rows = tab[0, K * T : K * T + 16 * T].rearrange("(q b) -> q b", q=16).bitcast(I32)
+        for i in range(4):
+            nc.scalar.dma_start(table_scales[:].bitcast(I32)[i:P:32, :], scale_rows[i:16:4, :])
+
+        w_rows = w.rearrange("(p t) n -> p t n", t=PACK)
+        w_raw = []
+        for h in range(M // LOAD_COLS):
+            raw = keep.tile([P, PACK, LOAD_COLS], F32, name=f"w_raw{h}")
+            nc.sync.dma_start(raw[:], w_rows[:, :, h * LOAD_COLS : (h + 1) * LOAD_COLS])
+            w_raw.append(raw)
+
+        residual = keep.tile([P, J_TILES, M], F32, name="residual")
+        nc.sync.dma_start(residual[:], r.rearrange("(jt p) n -> p jt n", p=P))
+
+        picked_scales = keep.tile([P, G * S], U8, name="picked_scales", align_bytes=64)
+        nc.vector.tensor_copy(picked_scales[:], table_scales[:].indirect(offsets[:]))
+        picked_words = keep.tile([P, G * S], U32, name="picked_words", align_bytes=64)
+        nc.vector.tensor_copy(picked_words[:], table_words[:].bitcast(U32).indirect(offsets[:]))
+
+        out_rows = out.rearrange("(jt p) n -> p jt n", p=P)
+        per_load = LOAD_COLS // CHUNK
+        results = [keep.tile([P, J_TILES, LOAD_COLS], F32, name=f"result{h}") for h in range(M // LOAD_COLS)]
+        accs = []
+        for c in range(M // CHUNK):
+            h, part = divmod(c, per_load)
+            grouped = keep.tile([P, CHUNK * PACK], BF16, name=f"grouped{c}", align_bytes=64)
+            dst = grouped[:].rearrange("p (c i t) -> p c t i", i=4, t=PACK)
+            src = w_raw[h][:, :, part * CHUNK : (part + 1) * CHUNK].rearrange("p t (c i) -> p c t i", i=4)
+            if part == 0:
+                nc.vector.tensor_copy(dst, src)
+            else:
+                nc.scalar.copy(dst, src)
+            w_words = keep.tile([P, CHUNK], U32, name=f"w_words{c}", align_bytes=64)
+            w_scales = keep.tile([P, CHUNK], U8, name=f"w_scales{c}", align_bytes=64)
+            nc.vector.quantize_mx(out=w_words[:].bitcast(FP8X4), scales=w_scales[:], in_=grouped[:])
+
+            acc = psum.tile([P, J_TILES, CHUNK], F32, name=f"acc{c}")
+            for jt in range(J_TILES):
+                for g in range(G):
+                    cols = slice(g * S + jt * P, g * S + (jt + 1) * P)
+                    nc.tensor.matmul_mx(
+                        out=acc[:, jt, :],
+                        lhsT=picked_words[:, cols].bitcast(FP8X4),
+                        lhsT_scale=picked_scales[:, cols],
+                        rhs=w_words[:].bitcast(FP8X4),
+                        rhs_scale=w_scales[:],
+                        start=(g == 0),
+                        stop=(g == G - 1),
+                    )
+            accs.append(acc)
+
+        for c in range(M // CHUNK):
+            h, part = divmod(c, per_load)
+            nc.vector.tensor_tensor(
+                results[h][:, :, part * CHUNK : (part + 1) * CHUNK],
+                accs[c][:],
+                residual[:, :, c * CHUNK : (c + 1) * CHUNK],
+                ADD,
+            )
+            if part == per_load - 1:
+                nc.sync.dma_start(out_rows[:, :, h * LOAD_COLS : (h + 1) * LOAD_COLS], results[h][:])

@@ -16,83 +16,103 @@ ADD = mybir.AluOpType.add
 
 P = 128
 PACK = 4
+BLOCKS = K // 32
+QUADRANT = 32
 J_TILES = S // P
-LOAD_COLS = 256
-CHUNK = 128
+HALF = M // 2
+QUARTER = M // 4
+LIST_COLS = S // 16
+FIRST_ON_VECTOR = 160
+HALF_BYTES = 4 * HALF
 
 
 def tile_list_tabbag_tm_res_kernel(tc, tab, w, r, offs, out):
     nc = tc.nc
     with ExitStack() as ctx:
         keep = ctx.enter_context(tc.tile_pool(name="keep", bufs=1))
+        reused = ctx.enter_context(tc.tile_pool(name="reused", bufs=1))
         psum = ctx.enter_context(tc.psum_pool(name="psum", bufs=1))
 
-        offsets = keep.tile([P, G * S // 16], U16, name="offsets")
-        nc.sync.dma_start(offsets[:], offs)
+        def load_w_half(h):
+            raw = keep.tile([P, PACK, HALF], F32, name=f"w_raw{h}")
+            nc.sync.dma_start(raw[:], w.rearrange("(p t) n -> p t n", t=PACK)[:, :, h * HALF : (h + 1) * HALF])
+            return raw
 
-        table_words = keep.tile([P, T], I32, name="table_words")
-        nc.sync.dma_start(table_words[:], tab[0, 0 : K * T].rearrange("(p b) -> p b", p=P).bitcast(I32))
+        def round_and_interleave(copy, grouped, raw):
+            copy(
+                grouped.rearrange("p (c i t) -> p c t i", i=4, t=PACK),
+                raw.rearrange("p t (c i) -> p c t i", i=4),
+            )
+
+        def quantise(grouped, width, name):
+            words = keep.tile([P, width], U32, name=f"w_words_{name}", align_bytes=64)
+            scales = keep.tile([P, width], U8, name=f"w_scales_{name}", align_bytes=64)
+            nc.vector.quantize_mx(out=words[:].bitcast(FP8X4), scales=scales[:], in_=grouped[:])
+            return words, scales
 
         table_scales = keep.tile([P, T], U8, name="table_scales")
         nc.vector.memset(table_scales[:].bitcast(I32), 0)
-        scale_rows = tab[0, K * T : K * T + 16 * T].rearrange("(q b) -> q b", q=16).bitcast(I32)
+
+        w_first = load_w_half(0)
+        offsets = keep.tile([P, G * LIST_COLS], U16, name="offsets")
+        nc.sync.dma_start(offsets[:], offs)
+        scale_rows = tab[0, K * T : (K + BLOCKS) * T].rearrange("(q b) -> q b", q=BLOCKS).bitcast(I32)
         for i in range(4):
-            nc.scalar.dma_start(table_scales[:].bitcast(I32)[i:P:32, :], scale_rows[i:16:4, :])
+            nc.sync.dma_start(table_scales[:].bitcast(I32)[i:P:QUADRANT, :], scale_rows[i:BLOCKS:4, :])
+        table_words = keep.tile([P, T], I32, name="table_words")
+        nc.sync.dma_start(table_words[:], tab[0, 0 : K * T].rearrange("(p b) -> p b", p=P).bitcast(I32))
+        w_second = load_w_half(1)
+        residual = []
+        for jt in range(J_TILES):
+            rows = keep.tile([P, M], F32, name=f"residual{jt}")
+            nc.sync.dma_start(rows[:], r[jt * P : (jt + 1) * P, :])
+            residual.append(rows)
 
-        w_rows = w.rearrange("(p t) n -> p t n", t=PACK)
-        w_raw = []
-        for h in range(M // LOAD_COLS):
-            raw = keep.tile([P, PACK, LOAD_COLS], F32, name=f"w_raw{h}")
-            nc.sync.dma_start(raw[:], w_rows[:, :, h * LOAD_COLS : (h + 1) * LOAD_COLS])
-            w_raw.append(raw)
-
-        residual = keep.tile([P, J_TILES, M], F32, name="residual")
-        nc.sync.dma_start(residual[:], r.rearrange("(jt p) n -> p jt n", p=P))
+        grouped_first = keep.tile([P, HALF * PACK], BF16, name="grouped_first", align_bytes=64)
+        split = FIRST_ON_VECTOR
+        round_and_interleave(nc.vector.tensor_copy, grouped_first[:, : split * PACK], w_first[:, :, :split])
+        round_and_interleave(nc.scalar.copy, grouped_first[:, split * PACK :], w_first[:, :, split:])
+        mx_first = quantise(grouped_first, HALF, "first")
 
         picked_scales = keep.tile([P, G * S], U8, name="picked_scales", align_bytes=64)
         nc.vector.tensor_copy(picked_scales[:], table_scales[:].indirect(offsets[:]))
-        picked_words = keep.tile([P, G * S], U32, name="picked_words", align_bytes=64)
-        nc.vector.tensor_copy(picked_words[:], table_words[:].bitcast(U32).indirect(offsets[:]))
+        picked_words = []
+        for g in range(G):
+            words = keep.tile([P, S], U32, name=f"picked_words{g}", align_bytes=64)
+            one_list = offsets[:, g * LIST_COLS : (g + 1) * LIST_COLS]
+            nc.vector.tensor_copy(words[:], table_words[:].bitcast(U32).indirect(one_list))
+            picked_words.append(words)
 
-        out_rows = out.rearrange("(jt p) n -> p jt n", p=P)
-        per_load = LOAD_COLS // CHUNK
-        results = [keep.tile([P, J_TILES, LOAD_COLS], F32, name=f"result{h}") for h in range(M // LOAD_COLS)]
-        accs = []
-        for c in range(M // CHUNK):
-            h, part = divmod(c, per_load)
-            grouped = keep.tile([P, CHUNK * PACK], BF16, name=f"grouped{c}", align_bytes=64)
-            dst = grouped[:].rearrange("p (c i t) -> p c t i", i=4, t=PACK)
-            src = w_raw[h][:, :, part * CHUNK : (part + 1) * CHUNK].rearrange("p t (c i) -> p c t i", i=4)
-            if part == 0:
-                nc.vector.tensor_copy(dst, src)
-            else:
-                nc.scalar.copy(dst, src)
-            w_words = keep.tile([P, CHUNK], U32, name=f"w_words{c}", align_bytes=64)
-            w_scales = keep.tile([P, CHUNK], U8, name=f"w_scales{c}", align_bytes=64)
-            nc.vector.quantize_mx(out=w_words[:].bitcast(FP8X4), scales=w_scales[:], in_=grouped[:])
-
-            acc = psum.tile([P, J_TILES, CHUNK], F32, name=f"acc{c}")
-            for jt in range(J_TILES):
-                for g in range(G):
-                    cols = slice(g * S + jt * P, g * S + (jt + 1) * P)
-                    nc.tensor.matmul_mx(
-                        out=acc[:, jt, :],
-                        lhsT=picked_words[:, cols].bitcast(FP8X4),
-                        lhsT_scale=picked_scales[:, cols],
-                        rhs=w_words[:].bitcast(FP8X4),
-                        rhs_scale=w_scales[:],
-                        start=(g == 0),
-                        stop=(g == G - 1),
-                    )
-            accs.append(acc)
-
-        for c in range(M // CHUNK):
-            h, part = divmod(c, per_load)
-            nc.vector.tensor_tensor(
-                results[h][:, :, part * CHUNK : (part + 1) * CHUNK],
-                accs[c][:],
-                residual[:, :, c * CHUNK : (c + 1) * CHUNK],
-                ADD,
+        def mx_pass(acc, jt, g, w_mx):
+            nc.tensor.matmul_mx(
+                out=acc,
+                lhsT=picked_words[g][:, jt * P : (jt + 1) * P].bitcast(FP8X4),
+                lhsT_scale=picked_scales[:, g * S + jt * P : g * S + (jt + 1) * P],
+                rhs=w_mx[0][:].bitcast(FP8X4),
+                rhs_scale=w_mx[1][:],
+                start=(g == 0),
+                stop=(g == G - 1),
             )
-            if part == per_load - 1:
-                nc.sync.dma_start(out_rows[:, :, h * LOAD_COLS : (h + 1) * LOAD_COLS], results[h][:])
+
+        sums = [[psum.tile([P, HALF], F32, name=f"sum{jt}_{h}") for h in range(2)] for jt in range(J_TILES)]
+        for g in range(G):
+            for jt in range(J_TILES):
+                mx_pass(sums[jt][0][:], jt, g, mx_first)
+
+        grouped_third = keep.tile([P, QUARTER * PACK], BF16, name="grouped_third", align_bytes=64)
+        grouped_fourth = reused.tile([P, QUARTER * PACK], BF16, name="grouped_fourth", align_bytes=64, offset=HALF_BYTES // 2)
+        round_and_interleave(nc.vector.tensor_copy, grouped_third[:], w_second[:, :, :QUARTER])
+        round_and_interleave(nc.scalar.copy, grouped_fourth[:], w_second[:, :, QUARTER:])
+        mx_second = [quantise(grouped_third, QUARTER, "third"), quantise(grouped_fourth, QUARTER, "fourth")]
+        for jt in range(J_TILES):
+            for part in range(2):
+                for g in range(G):
+                    mx_pass(sums[jt][1][:, part * QUARTER : (part + 1) * QUARTER], jt, g, mx_second[part])
+
+        for h in range(2):
+            cols = slice(h * HALF, (h + 1) * HALF)
+            for jt in range(J_TILES):
+                place = (h * J_TILES + jt) * HALF_BYTES
+                result = reused.tile([P, HALF], F32, name=f"result{jt}_{h}", align_bytes=64, offset=place)
+                nc.vector.tensor_tensor(result[:], sums[jt][h][:], residual[jt][:, cols], ADD)
+                nc.sync.dma_start(out[jt * P : (jt + 1) * P, cols], result[:])

from contextlib import ExitStack

import concourse.mybir as mybir

G, K, M, T, S = 2, 512, 512, 2048, 256
FLOPS = 2 * G * K * M * S

F32 = mybir.dt.float32
BF16 = mybir.dt.bfloat16
I32 = mybir.dt.int32
U32 = mybir.dt.uint32
U16 = mybir.dt.uint16
U8 = mybir.dt.uint8
FP8X4 = mybir.dt.float8_e4m3fn_x4
ADD = mybir.AluOpType.add

P = 128
PACK = 4
BLOCKS = K // 32
QUADRANT = 32
J_TILES = S // P
HALF = M // 2
QUARTER = M // 4
LIST_COLS = S // 16
FIRST_ON_VECTOR = 160
HALF_BYTES = 4 * HALF


def tile_list_tabbag_tm_res_kernel(tc, tab, w, r, offs, out):
    nc = tc.nc
    with ExitStack() as ctx:
        keep = ctx.enter_context(tc.tile_pool(name="keep", bufs=1))
        reused = ctx.enter_context(tc.tile_pool(name="reused", bufs=1))
        psum = ctx.enter_context(tc.psum_pool(name="psum", bufs=1))

        def load_w_half(h):
            raw = keep.tile([P, PACK, HALF], F32, name=f"w_raw{h}")
            nc.sync.dma_start(raw[:], w.rearrange("(p t) n -> p t n", t=PACK)[:, :, h * HALF : (h + 1) * HALF])
            return raw

        def round_and_interleave(copy, grouped, raw):
            copy(
                grouped.rearrange("p (c i t) -> p c t i", i=4, t=PACK),
                raw.rearrange("p t (c i) -> p c t i", i=4),
            )

        def quantise(grouped, width, name):
            words = keep.tile([P, width], U32, name=f"w_words_{name}", align_bytes=64)
            scales = keep.tile([P, width], U8, name=f"w_scales_{name}", align_bytes=64)
            nc.vector.quantize_mx(out=words[:].bitcast(FP8X4), scales=scales[:], in_=grouped[:])
            return words, scales

        table_scales = keep.tile([P, T], U8, name="table_scales")
        nc.vector.memset(table_scales[:].bitcast(I32), 0)

        w_first = load_w_half(0)
        offsets = keep.tile([P, G * LIST_COLS], U16, name="offsets")
        nc.sync.dma_start(offsets[:], offs)
        scale_rows = tab[0, K * T : (K + BLOCKS) * T].rearrange("(q b) -> q b", q=BLOCKS).bitcast(I32)
        for i in range(4):
            nc.sync.dma_start(table_scales[:].bitcast(I32)[i:P:QUADRANT, :], scale_rows[i:BLOCKS:4, :])
        table_words = keep.tile([P, T], I32, name="table_words")
        nc.sync.dma_start(table_words[:], tab[0, 0 : K * T].rearrange("(p b) -> p b", p=P).bitcast(I32))
        w_second = load_w_half(1)
        residual = []
        for jt in range(J_TILES):
            rows = keep.tile([P, M], F32, name=f"residual{jt}")
            nc.sync.dma_start(rows[:], r[jt * P : (jt + 1) * P, :])
            residual.append(rows)

        grouped_first = keep.tile([P, HALF * PACK], BF16, name="grouped_first", align_bytes=64)
        split = FIRST_ON_VECTOR
        round_and_interleave(nc.vector.tensor_copy, grouped_first[:, : split * PACK], w_first[:, :, :split])
        round_and_interleave(nc.scalar.copy, grouped_first[:, split * PACK :], w_first[:, :, split:])
        mx_first = quantise(grouped_first, HALF, "first")

        picked_scales = keep.tile([P, G * S], U8, name="picked_scales", align_bytes=64)
        nc.vector.tensor_copy(picked_scales[:], table_scales[:].indirect(offsets[:]))
        picked_words = []
        for g in range(G):
            words = keep.tile([P, S], U32, name=f"picked_words{g}", align_bytes=64)
            one_list = offsets[:, g * LIST_COLS : (g + 1) * LIST_COLS]
            nc.vector.tensor_copy(words[:], table_words[:].bitcast(U32).indirect(one_list))
            picked_words.append(words)

        def mx_pass(acc, jt, g, w_mx):
            nc.tensor.matmul_mx(
                out=acc,
                lhsT=picked_words[g][:, jt * P : (jt + 1) * P].bitcast(FP8X4),
                lhsT_scale=picked_scales[:, g * S + jt * P : g * S + (jt + 1) * P],
                rhs=w_mx[0][:].bitcast(FP8X4),
                rhs_scale=w_mx[1][:],
                start=(g == 0),
                stop=(g == G - 1),
            )

        sums = [[psum.tile([P, HALF], F32, name=f"sum{jt}_{h}") for h in range(2)] for jt in range(J_TILES)]
        for g in range(G):
            for jt in range(J_TILES):
                mx_pass(sums[jt][0][:], jt, g, mx_first)

        grouped_third = keep.tile([P, QUARTER * PACK], BF16, name="grouped_third", align_bytes=64)
        grouped_fourth = reused.tile([P, QUARTER * PACK], BF16, name="grouped_fourth", align_bytes=64, offset=HALF_BYTES // 2)
        round_and_interleave(nc.vector.tensor_copy, grouped_third[:], w_second[:, :, :QUARTER])
        round_and_interleave(nc.scalar.copy, grouped_fourth[:], w_second[:, :, QUARTER:])
        mx_second = [quantise(grouped_third, QUARTER, "third"), quantise(grouped_fourth, QUARTER, "fourth")]
        for jt in range(J_TILES):
            for part in range(2):
                for g in range(G):
                    mx_pass(sums[jt][1][:, part * QUARTER : (part + 1) * QUARTER], jt, g, mx_second[part])

        for h in range(2):
            cols = slice(h * HALF, (h + 1) * HALF)
            for jt in range(J_TILES):
                place = (h * J_TILES + jt) * HALF_BYTES
                result = reused.tile([P, HALF], F32, name=f"result{jt}_{h}", align_bytes=64, offset=place)
                nc.vector.tensor_tensor(result[:], sums[jt][h][:], residual[jt][:, cols], ADD)
                nc.sync.dma_start(out[jt * P : (jt + 1) * P, cols], result[:])
